import numpy as np
import ml_dtypes


def mxq(x, axis, fmt="e4m3"):
    dtype, down = {"e4m3": (ml_dtypes.float8_e4m3fn, 7), "e5m2": (ml_dtypes.float8_e5m2, 14)}[fmt]
    v = np.moveaxis(np.asarray(x, np.float32).astype(ml_dtypes.bfloat16).astype(np.float64), axis, -1)
    blocks = v.reshape(v.shape[:-1] + (-1, 32))
    amax = np.abs(blocks).max(-1, keepdims=True)
    byte = np.maximum(np.where(amax > 0, np.frexp(amax)[1] - 1 + 127, 0) - down, 1)
    scale = np.exp2(byte - 127.0)
    codes = (blocks / scale).astype(np.float32).astype(dtype).astype(np.float64)
    return np.moveaxis((codes * scale).reshape(v.shape), -1, axis)


WIDE = False


def mx_kscale(k):
    if not WIDE:
        return np.ones(k)
    levels = np.array([10, -10, 5, -5, 0])
    if k % 512:
        return np.exp2(np.random.permutation(np.resize(levels, k // 32))).repeat(32)
    a = np.empty((k // 512, 16))
    for p in range(k // 512):
        a[p, :8] = np.random.permutation(np.resize(levels, 8))
        for g in range(8):
            far = levels[np.abs(levels - a[p, g]) >= 10]
            a[p, g + 8] = far[np.random.randint(len(far))]
    return np.exp2(a.ravel()).repeat(32)


BF16 = ml_dtypes.bfloat16


def bf(x):
    return np.asarray(x, np.float32).astype(BF16)


def f64(x):
    return np.asarray(x).astype(np.float64)


E2M1 = np.array([0.0, 0.5, 1.0, 1.5, 2.0, 3.0, 4.0, 6.0, -0.0, -0.5, -1.0, -1.5, -2.0, -3.0, -4.0, -6.0])


def pack_weight(w, fmt):
    k, n = w.shape
    w = f64(bf(w)).reshape(k // 32, 32, n)
    amax = np.abs(w).max(1)
    if fmt == "e4m3":
        byte = np.frexp(amax)[1] - 1 + 127 - 7
    else:
        mant, ex = np.frexp(amax / 6.0)
        byte = np.where(mant > 0.5, ex, ex - 1) + 127
    byte = np.clip(np.where(amax > 0, byte, 1), 1, 254)
    scaled = (w * np.exp2(127.0 - byte)[:, None, :]).reshape(k, n).astype(np.float32)
    by_word = np.ascontiguousarray(scaled.reshape(k // 512, 128, 4, n).transpose(0, 1, 3, 2))
    if fmt == "e4m3":
        words = by_word.astype(ml_dtypes.float8_e4m3fn).view(np.uint8)
    else:
        c = by_word.astype(ml_dtypes.float4_e2m1fn).view(np.uint8) & 0xF
        words = c[..., 0::2] | (c[..., 1::2] << 4)
    return np.ascontiguousarray(words), np.ascontiguousarray(byte.astype(np.uint8).reshape(k // 512, 16, n))


def unpack_weight(words, scales, fmt):
    g, p, n, _ = words.shape
    if fmt == "e4m3":
        vals = np.ascontiguousarray(words).view(ml_dtypes.float8_e4m3fn).astype(np.float64)
    else:
        nib = np.empty((g, p, n, 4), np.uint8)
        nib[..., 0::2] = words & 0xF
        nib[..., 1::2] = words >> 4
        vals = E2M1[nib]
    vals = vals * np.repeat(np.exp2(scales.astype(np.float64) - 127.0), 8, axis=1)[..., None]
    return vals.transpose(0, 1, 3, 2).reshape(g * 512, n)
def pack4(w):
    words, scales = pack_weight(w, "e2m1")
    return words.reshape(words.shape[0], 128, -1), scales


def unpack4(words, scales):
    return unpack_weight(words.reshape(words.shape[0], 128, -1, 2), scales, "e2m1")


M, K, N, R = 2048, 1024, 2048, 256


def draw0():
    s = mx_kscale(K)
    u = mx_kscale(M)
    keep = 1.0 * (np.fft.rfft(np.random.standard_normal(K)).real > 0)
    flip = np.sign(np.random.standard_normal((K, 1)))
    both = np.concatenate([np.eye(K), np.random.standard_normal((K, R)) / np.sqrt(K)], axis=1)
    both = flip * np.fft.irfft(keep[:, None] * np.fft.rfft(flip * both, axis=0), axis=0)
    e_words, e_scales = pack4(np.random.standard_normal((M, R)) / np.sqrt(M) / u[:, None])
    d_words, d_scales = pack4(np.random.standard_normal((M, N)) / np.sqrt(M) / u[:, None])
    return {"x": bf(np.random.standard_normal((M, K)) * s),
            "proj": bf(both[:, :K] / s[:, None]),
            "a": bf(both[:, K:] / s[:, None]),
            "r": bf((1 + 0.3 * np.random.standard_normal(M)) * u),
            "e_words": e_words, "e_scales": e_scales,
            "d_words": d_words, "d_scales": d_scales}


def core(x, proj, a, r, e_words, e_scales, d_words, d_scales):
    xq = mxq(f64(x), 1, "e4m3")
    rw = f64(r)[:, None]
    xh = (xq @ mxq(f64(proj), 0, "e4m3")) * rw
    z = (xq @ mxq(f64(a), 0, "e4m3")) * rw
    grad_a = mxq(xh, 0, "e4m3").T @ unpack4(e_words, e_scales)
    grad_b = mxq(z, 0, "e4m3").T @ unpack4(d_words, d_scales)
    return grad_a, grad_b


def e4m3fn_bytes(y):
    return np.clip(np.asarray(y, np.float64), -448.0, 448.0).astype(np.float32).astype(ml_dtypes.float8_e4m3fn).view(np.uint8)


def e4m3fn_values(b):
    return np.asarray(b, np.uint8).view(ml_dtypes.float8_e4m3fn).astype(np.float64)


def setup_inputs():
    d = draw0()
    x0 = np.asarray(d['x']).astype(np.float64)
    s = (np.max(np.abs(x0), axis=(0,), keepdims=True) / 448.0).astype(np.float32)
    out = {}
    for k, v in d.items():
        if k == 'x':
            out['x_bytes'] = e4m3fn_bytes(x0 / s.astype(np.float64))
            out['x_scale'] = s
        else:
            out[k] = v
    return out


def reference(x_bytes, x_scale, proj, a, r, e_words, e_scales, d_words, d_scales):
    return core(e4m3fn_values(x_bytes) * x_scale.astype(np.float64), proj, a, r, e_words, e_scales, d_words, d_scales)

@@ -1,0 +1,329 @@
+from contextlib import ExitStack
+
+import concourse.mybir as mybir
+from concourse.masks import make_identity
+
+M, K, N, R = 2048, 1024, 2048, 256
+FLOPS = 2 * M * K * (K + R) + 2 * K * M * R + 2 * R * M * N
+
+F32 = mybir.dt.float32
+BF16 = mybir.dt.bfloat16
+I32 = mybir.dt.int32
+U32 = mybir.dt.uint32
+U8 = mybir.dt.uint8
+E4M3 = mybir.dt.float8_e4m3fn
+E4M3X4 = mybir.dt.float8_e4m3fn_x4
+E2M1X4 = mybir.dt.float4_e2m1fn_x4
+MULT = mybir.AluOpType.mult
+COPY = mybir.ActivationFunctionType.Copy
+
+P = 128
+T4 = 4
+GROUP = P * T4
+GROUPS = M // GROUP
+KP = K // GROUP
+HALF = 512
+
+
+def tile_protected_adapter_gradients_s13_kernel(
+    tc, x_bytes, x_scale, proj, a, r, e_words, e_scales, d_words, d_scales, out_0, out_1
+):
+    nc = tc.nc
+    with ExitStack() as ctx:
+        keep = ctx.enter_context(tc.tile_pool(name="keep", bufs=1))
+        xin = ctx.enter_context(tc.tile_pool(name="xin", bufs=4))
+        xbp = ctx.enter_context(tc.tile_pool(name="xbp", bufs=3))
+        xgp = ctx.enter_context(tc.tile_pool(name="xgp", bufs=3))
+        grp = ctx.enter_context(tc.tile_pool(name="grp", bufs=2))
+        outp = ctx.enter_context(tc.tile_pool(name="outp", bufs=4))
+        ps_tr = ctx.enter_context(tc.psum_pool(name="ps_tr", bufs=2))
+        ps_z = ctx.enter_context(tc.psum_pool(name="ps_z", bufs=1))
+        ps_mm = ctx.enter_context(tc.psum_pool(name="ps_mm", bufs=4))
+
+        warm = keep.tile([P, 1], F32, name="warm")
+        nc.gpsimd.memset(warm[:], 0.0)
+        nc.scalar.activation(out=warm[:], in_=warm[:], func=COPY)
+        ident = keep.tile([P, P], F32, name="ident")
+        make_identity(nc, ident[:])
+        es = keep.tile([P, GROUPS, R], U8, name="es", align_bytes=64)
+        ds = keep.tile([P, GROUPS, N], U8, name="ds", align_bytes=64)
+        nc.gpsimd.memset(es[:].rearrange("p g n -> p (g n)").bitcast(I32), 0)
+        nc.gpsimd.memset(ds[:].rearrange("p g n -> p (g n)").bitcast(I32), 0)
+
+        r16 = keep.tile([P, GROUPS, T4], BF16, name="r16")
+        nc.scalar.dma_start(out=r16[:], in_=r.rearrange("(g p t) -> p g t", p=P, t=T4))
+        r32 = keep.tile([P, GROUPS, T4], F32, name="r32")
+        nc.gpsimd.tensor_copy(out=r32[:], in_=r16[:])
+
+        proj_v = proj.rearrange("(a p j) n -> a p j n", p=P, j=T4)
+        xb_v = x_bytes.rearrange("(g p t) k -> g p t k", p=P, t=T4)
+        praw = {}
+
+        def load_proj(c, kp):
+            w = keep.tile([P, T4, HALF], BF16, name="praw%d%d" % (c, kp))
+            nc.sync.dma_start(out=w[:], in_=proj_v[kp, :, :, c * HALF : (c + 1) * HALF])
+            praw[c, kp] = w
+
+        xs = keep.tile([P, K], F32, name="xs")
+        x_in = {}
+
+        def load_x(g):
+            xt = xin.tile([P, T4, K], U8, name="x_in")
+            nc.sync.dma_start(out=xt[:], in_=xb_v[g])
+            x_in[g] = xt
+
+        load_proj(0, 0)
+        nc.sync.dma_start(out=xs[:], in_=x_scale.rearrange("o k -> (o k)").partition_broadcast(P))
+        load_x(0)
+        load_proj(0, 1)
+        araw = keep.tile([P, KP, T4, R], BF16, name="araw")
+        nc.sync.dma_start(out=araw[:], in_=a.rearrange("(a p j) n -> p a j n", p=P, j=T4))
+        load_proj(1, 0)
+        load_proj(1, 1)
+        for g in range(1, GROUPS):
+            load_x(g)
+        ew = keep.tile([P, GROUPS, 2 * R], U8, name="ew", align_bytes=64)
+        dw = keep.tile([P, GROUPS, 2 * N], U8, name="dw", align_bytes=64)
+        for g in range(GROUPS):
+            nc.sync.dma_start(out=dw[:, g, :].bitcast(I32), in_=d_words[g].bitcast(I32))
+        nc.sync.dma_start(out=ew[:].bitcast(I32), in_=e_words.bitcast(I32).rearrange("g p n -> p g n"))
+        for q in range(4):
+            nc.sync.dma_start(
+                out=ds[32 * q : 32 * q + 4].bitcast(I32),
+                in_=d_scales[:, 4 * q : 4 * q + 4, :].bitcast(I32).rearrange("g q n -> q g n"),
+            )
+            nc.sync.dma_start(
+                out=es[32 * q : 32 * q + 4].bitcast(I32),
+                in_=e_scales[:, 4 * q : 4 * q + 4, :].bitcast(I32).rearrange("g q n -> q g n"),
+            )
+
+        pq = keep.tile([P, 2, KP, HALF], U32, name="pq", align_bytes=64)
+        pqs = keep.tile([P, 2, KP, HALF], U8, name="pqs", align_bytes=64)
+        aq = keep.tile([P, KP, R], U32, name="aq", align_bytes=64)
+        aqs = keep.tile([P, KP, R], U8, name="aqs", align_bytes=64)
+        xq = keep.tile([P, GROUPS, T4, KP, P], U32, name="xq", align_bytes=64)
+        xqs = keep.tile([P, GROUPS, T4, KP, P], U8, name="xqs", align_bytes=64)
+        zq = keep.tile([P, GROUPS, R], U32, name="zq", align_bytes=64)
+        zqs = keep.tile([P, GROUPS, R], U8, name="zqs", align_bytes=64)
+        hq = keep.tile([P, GROUPS, K], U32, name="hq", align_bytes=64)
+        hqs = keep.tile([P, GROUPS, K], U8, name="hqs", align_bytes=64)
+
+        def mx(out, lhs, lhs_s, rhs, rhs_s, start, stop, rdt=E4M3X4):
+            nc.tensor.matmul_mx(
+                out=out,
+                lhsT=lhs.bitcast(E4M3X4),
+                lhsT_scale=lhs_s,
+                rhs=rhs.bitcast(rdt),
+                rhs_scale=rhs_s,
+                start=start,
+                stop=stop,
+            )
+
+        pgr = {}
+
+        def proj_inter(c, kp, eng):
+            w = keep.tile([P, HALF, T4], BF16, name="pgr%d%d" % (c, kp), align_bytes=64)
+            eng(out=w[:], in_=praw[c, kp][:].rearrange("p j n -> p n j"))
+            pgr[c, kp] = w
+
+        def proj_quant(c, kp):
+            nc.vector.quantize_mx(
+                out=pq[:, c, kp, :].bitcast(E4M3X4),
+                scales=pqs[:, c, kp, :],
+                in_=pgr[c, kp][:].rearrange("p n j -> p (n j)"),
+            )
+
+        x_bf = {}
+
+        def x_mult(g, t):
+            w = xbp.tile([P, K], BF16, name="x_bf")
+            nc.vector.tensor_tensor(out=w[:], in0=x_in[g][:, t, :].bitcast(E4M3), in1=xs[:], op=MULT)
+            x_bf[g, t] = w
+
+        x_gr = {}
+
+        def x_turn(g, t):
+            bank = ps_tr.tile([P, KP, 2, P], F32, name="bank_tr")
+            words = x_bf[g, t][:].bitcast(F32)
+            for kp in range(KP):
+                for u in range(2):
+                    nc.tensor.transpose(bank[:, kp, u, :], words[:, 256 * kp + u : 256 * (kp + 1) : 2], ident[:])
+            w = xgp.tile([P, KP, P, T4], BF16, name="x_gr", align_bytes=64)
+            nc.scalar.copy(
+                out=w[:].rearrange("p a r j -> p (a r j)").bitcast(F32).rearrange("p (a r u) -> p a r u", a=KP, u=2),
+                in_=bank[:].rearrange("p a u r -> p a r u"),
+            )
+            x_gr[g, t] = w
+
+        def x_quant(g, t):
+            nc.vector.quantize_mx(
+                out=xq[:, g, t].rearrange("p a r -> p (a r)").bitcast(E4M3X4),
+                scales=xqs[:, g, t].rearrange("p a r -> p (a r)"),
+                in_=x_gr[g, t][:].rearrange("p a r j -> p (a r j)"),
+            )
+
+        z_bank = {}
+
+        def z_mm(g, t):
+            for h in range(2):
+                if t == 0:
+                    z_bank[h] = ps_z.tile([P, T4, P], F32, name="z_bank%d" % h)
+                for kp in range(KP):
+                    mx(
+                        z_bank[h][:, t, :],
+                        xq[:, g, t, kp, :],
+                        xqs[:, g, t, kp, :],
+                        aq[:, kp, h * P : (h + 1) * P],
+                        aqs[:, kp, h * P : (h + 1) * P],
+                        kp == 0,
+                        kp == KP - 1,
+                    )
+
+        z_gr = {}
+
+        def z_out(g):
+            w = grp.tile([P, R, T4], BF16, name="z_gr", align_bytes=64)
+            for h in range(2):
+                nc.vector.tensor_tensor(
+                    out=w[:, h * P : (h + 1) * P, :],
+                    in0=z_bank[h][:].rearrange("p t n -> p n t"),
+                    in1=r32[:, g : g + 1, :].to_broadcast([P, P, T4]),
+                    op=MULT,
+                )
+            z_gr[g] = w
+
+        def z_quant(g):
+            nc.vector.quantize_mx(
+                out=zq[:, g, :].bitcast(E4M3X4), scales=zqs[:, g, :], in_=z_gr[g][:].rearrange("p n t -> p (n t)")
+            )
+
+        h_pl = {}
+
+        def h_mm(g, t, c):
+            bank = ps_mm.tile([P, HALF], F32, name="bank_mm")
+            for kp in range(KP):
+                mx(
+                    bank[:],
+                    xq[:, g, t, kp, :],
+                    xqs[:, g, t, kp, :],
+                    pq[:, c, kp, :],
+                    pqs[:, c, kp, :],
+                    kp == 0,
+                    kp == KP - 1,
+                )
+            if t == 0:
+                h_pl[g, c] = grp.tile([P, T4, HALF], BF16, name="h_pl%d" % c)
+            nc.scalar.activation(out=h_pl[g, c][:, t, :], in_=bank[:], func=COPY, scale=r32[:, g, t : t + 1])
+
+        h_gr = {}
+
+        def h_inter(g, c):
+            w = grp.tile([P, HALF, T4], BF16, name="h_gr%d" % c, align_bytes=64)
+            nc.vector.tensor_copy(
+                out=w[:].rearrange("p (n i) t -> p n t i", i=4),
+                in_=h_pl[g, c][:].rearrange("p t (n i) -> p n t i", i=4),
+            )
+            h_gr[g, c] = w
+
+        def h_quant(g, c):
+            nc.vector.quantize_mx(
+                out=hq[:, g, c * HALF : (c + 1) * HALF].bitcast(E4M3X4),
+                scales=hqs[:, g, c * HALF : (c + 1) * HALF],
+                in_=h_gr[g, c][:].rearrange("p n t -> p (n t)"),
+            )
+
+        proj_inter(0, 0, nc.vector.tensor_copy)
+        proj_inter(0, 1, nc.scalar.copy)
+        x_mult(0, 0)
+        x_turn(0, 0)
+        proj_quant(0, 0)
+        x_mult(0, 1)
+        x_turn(0, 1)
+        x_quant(0, 0)
+        proj_quant(0, 1)
+        a_gr = keep.tile([P, KP, R, T4], BF16, name="a_gr", align_bytes=64)
+        nc.vector.tensor_copy(out=a_gr[:], in_=araw[:].rearrange("p a j n -> p a n j"))
+        proj_inter(1, 0, nc.scalar.copy)
+        proj_inter(1, 1, nc.scalar.copy)
+        nc.vector.quantize_mx(
+            out=aq[:].rearrange("p a n -> p (a n)").bitcast(E4M3X4),
+            scales=aqs[:].rearrange("p a n -> p (a n)"),
+            in_=a_gr[:].rearrange("p a n j -> p (a n j)"),
+        )
+        proj_quant(1, 0)
+        proj_quant(1, 1)
+
+        steps = [(g, t) for g in range(GROUPS) for t in range(T4)]
+        lead = 6
+        for i in range(2, len(steps) + lead):
+            if i < len(steps):
+                x_mult(*steps[i])
+                x_turn(*steps[i])
+            if 1 <= i - 1 < len(steps):
+                x_quant(*steps[i - 1])
+            j = i - lead
+            if j >= 0:
+                g, t = steps[j]
+                z_mm(g, t)
+                for c in range(2):
+                    h_mm(g, t, c)
+                if t == T4 - 1:
+                    z_out(g)
+                    z_quant(g)
+            j = i - lead - T4
+            if j >= 0:
+                g, t = steps[j]
+                if t == 0:
+                    h_inter(g, 0)
+                elif t == 1:
+                    h_inter(g, 1)
+                elif t == 2:
+                    h_quant(g, 0)
+                else:
+                    h_quant(g, 1)
+
+        for c in range(2):
+            h_inter(GROUPS - 1, c)
+        for c in range(2):
+            h_quant(GROUPS - 1, c)
+
+        for rb in range(R // P):
+            for nb in range(N // HALF):
+                bank = ps_mm.tile([P, HALF], F32, name="bank_mm")
+                for g in range(GROUPS):
+                    mx(
+                        bank[:],
+                        zq[:, g, rb * P : (rb + 1) * P],
+                        zqs[:, g, rb * P : (rb + 1) * P],
+                        dw[:, g, 2 * HALF * nb : 2 * HALF * (nb + 1)],
+                        ds[:, g, HALF * nb : HALF * (nb + 1)],
+                        g == 0,
+                        g == GROUPS - 1,
+                        E2M1X4,
+                    )
+                w = outp.tile([P, HALF], F32, name="res")
+                nc.scalar.copy(out=w[:], in_=bank[:])
+                nc.sync.dma_start(out=out_1[rb * P : (rb + 1) * P, nb * HALF : (nb + 1) * HALF], in_=w[:])
+
+        for kk in range(K // 256):
+            bank = ps_mm.tile([P, 2, R], F32, name="bank_mm")
+            for b in range(2):
+                k0 = kk * 256 + b * P
+                for h in range(2):
+                    for g in range(GROUPS):
+                        mx(
+                            bank[:, b, h * P : (h + 1) * P],
+                            hq[:, g, k0 : k0 + P],
+                            hqs[:, g, k0 : k0 + P],
+                            ew[:, g, 2 * P * h : 2 * P * (h + 1)],
+                            es[:, g, P * h : P * (h + 1)],
+                            g == 0,
+                            g == GROUPS - 1,
+                            E2M1X4,
+                        )
+            w = outp.tile([P, 2, R], F32, name="res")
+            if kk % 2 == 0:
+                nc.scalar.copy(out=w[:], in_=bank[:])
+            else:
+                nc.vector.tensor_copy(out=w[:], in_=bank[:])
+            nc.sync.dma_start(out=out_0[kk * 256 : (kk + 1) * 256, :].rearrange("(b p) n -> p b n", p=P), in_=w[:])

@@ -25,30 +25,54 @@ KP = K // GROUP
 HALF = 512
 
 
+ORDER = """
+XS:0 PI:00.V.- PT:01.0 PQ:00 PT:01.1 XM:0 PE:01.0 PE:01.1 XM:1 PI:a.S.0 TR:0 PI:a.S.1 PQ:01 TR:1
+PI:a.S.2 XM:2 PI:a.S.3 EV:0 PQ:a EV:1 XQ:0 TR:2 XM:3 PI:10.S.0 H:0.0 PI:10.S.1 Z:0 XQ:1 PI:10.S.2
+XM:4 H:1.0 PI:10.S.3 Z:1 XM:5 EV:2 TR:3 XE:0.0 TR:4 PQ:10 XE:1.0 XQ:2 EV:3 TR:5 XM:6 EV:4 H:2.0
+PI:11.S.0 Z:2 XQ:3 XQ:4 PI:11.S.1 H:3.0 XM:7 PI:11.S.2 Z:3 H:4.0 PI:11.S.3 ZE:0.0 TR:6 XE:2.0 PQ:11
+TR:7 XE:3.0 ZE:0.1 H:0.1 XE:4.0 XI:0.0 H:1.1 EV:5 H:2.1 XE:0.1 ZQ:0 Z:4 XE:1.1 XQ:5 H:3.1 XM:8
+XE:2.1 Z:5 H:5.0 XE:3.1 H:4.1 XM:9 EV:6 H:5.1 XE:5.0 XQ:6 TR:8 XM:10 XE:4.1 TR:9 XE:5.1 Z:6 XM:11
+EV:7 H:6.0 EV:8 H:6.1 XQ:7 XE:6.0 TR:10 XQ:8 XM:12 XE:6.1 TR:11 EV:9 Z:7 XM:13 H:7.0 EV:10 H:8.0
+EV:11 ZE:1.0 H:7.1 XE:7.0 ZE:1.1 XE:8.0 TR:12 XQ:9 TR:13 XE:7.1 ZQ:1 XQ:10 Z:8 EV:12 XM:14 H:9.0
+EV:13 Z:9 H:8.1 XE:9.0 XQ:11 XI:0.1 Z:10 H:10.0 XE:8.1 Z:11 XE:10.0 H:9.1 XM:15 H:11.0 XE:9.1 H:10.1
+ZE:2.0 XE:11.0 H:11.1 ZE:2.1 XE:10.1 TR:14 XQ:12 XE:11.1 ZQ:2 TR:15 XQ:13 EV:14 XI:1.0 Z:12 H:12.0
+EV:15 Z:13 XE:12.0 H:13.0 XQ:14 XQ:15 Z:14 XI:1.1 XE:13.0 H:12.1 Z:15 XE:12.1 H:14.0 ZE:3.0 H:13.1
+ZE:3.1 XE:14.0 H:15.0 HQ:0.0 XE:13.1 H:14.1 XE:15.0 ZQ:3 H:15.1 HQ:0.1 XE:14.1 GB:0 XI:2.0 XE:15.1
+GB:1 GBO:0.S HQ:1.0 GB:2 HQ:1.1 GBO:1.S XI:2.1 GB:3 GBO:2.S HQ:2.0 GB:4 GBO:3.S HQ:2.1 XI:3.0 GB:5
+GBO:4.S GB:6 XI:3.1a GBO:5.S HQ:3.0 GB:7 GBO:6.S HQ:3.1a XI:3.1b GA:0 GBO:7.S HQ:3.1b GA:1 GAO:0.S
+GA:2 GAO:1.V GA:3 GAO:2.S GAO:3.V
+"""
+
+
 def tile_protected_adapter_gradients_s13_kernel(
     tc, x_bytes, x_scale, proj, a, r, e_words, e_scales, d_words, d_scales, out_0, out_1
 ):
     nc = tc.nc
     with ExitStack() as ctx:
         keep = ctx.enter_context(tc.tile_pool(name="keep", bufs=1))
-        xin = ctx.enter_context(tc.tile_pool(name="xin", bufs=4))
-        xbp = ctx.enter_context(tc.tile_pool(name="xbp", bufs=3))
-        xgp = ctx.enter_context(tc.tile_pool(name="xgp", bufs=3))
+        xbp = ctx.enter_context(tc.tile_pool(name="xbp", bufs=8))
+        xgp = ctx.enter_context(tc.tile_pool(name="xgp", bufs=8))
+        hpl = ctx.enter_context(tc.tile_pool(name="hpl", bufs=3))
         grp = ctx.enter_context(tc.tile_pool(name="grp", bufs=2))
-        outp = ctx.enter_context(tc.tile_pool(name="outp", bufs=4))
-        ps_tr = ctx.enter_context(tc.psum_pool(name="ps_tr", bufs=2))
+        outp = ctx.enter_context(tc.tile_pool(name="outp", bufs=6))
+        ps_tr = ctx.enter_context(tc.psum_pool(name="ps_tr", bufs=3))
         ps_z = ctx.enter_context(tc.psum_pool(name="ps_z", bufs=1))
-        ps_mm = ctx.enter_context(tc.psum_pool(name="ps_mm", bufs=4))
+        ps_mm = ctx.enter_context(tc.psum_pool(name="ps_mm", bufs=3))
 
         warm = keep.tile([P, 1], F32, name="warm")
         nc.gpsimd.memset(warm[:], 0.0)
         nc.scalar.activation(out=warm[:], in_=warm[:], func=COPY)
         ident = keep.tile([P, P], F32, name="ident")
         make_identity(nc, ident[:])
+        ident16 = keep.tile([P, P], BF16, name="ident16")
+        nc.gpsimd.tensor_copy(out=ident16[:], in_=ident[:])
         es = keep.tile([P, GROUPS, R], U8, name="es", align_bytes=64)
         ds = keep.tile([P, GROUPS, N], U8, name="ds", align_bytes=64)
         nc.gpsimd.memset(es[:].rearrange("p g n -> p (g n)").bitcast(I32), 0)
         nc.gpsimd.memset(ds[:].rearrange("p g n -> p (g n)").bitcast(I32), 0)
+
+        sc_rows = keep.tile([P, P], F32, name="sc_rows")
+        nc.vector.memset(sc_rows[:], 0.0)
 
         r16 = keep.tile([P, GROUPS, T4], BF16, name="r16")
         nc.scalar.dma_start(out=r16[:], in_=r.rearrange("(g p t) -> p g t", p=P, t=T4))
@@ -64,18 +88,39 @@ def tile_protected_adapter_gradients_s13_kernel(
             nc.sync.dma_start(out=w[:], in_=proj_v[kp, :, :, c * HALF : (c + 1) * HALF])
             praw[c, kp] = w
 
-        xs = keep.tile([P, K], F32, name="xs")
+        xs = keep.tile([P, 2, HALF], F32, name="xs")
+        sc_col = keep.tile([P, K // P], F32, name="sc_col")
+
+        def spread_scales():
+            bank = ps_tr.tile([P, P], F32, name="bank_tr")
+            nc.tensor.transpose(bank[:], sc_rows[:], ident[:])
+            nc.scalar.copy(out=sc_col[:], in_=bank[:, 0 : K // P])
+            for b in range(2):
+                bank = ps_mm.tile([P, HALF], F32, name="bank_mm")
+                for j in range(HALF // P):
+                    m = b * (HALF // P) + j
+                    nc.tensor.transpose(
+                        bank[:, j * P : (j + 1) * P], sc_col[:, m : m + 1].to_broadcast([P, P]), ident[:]
+                    )
+                nc.scalar.copy(out=xs[:, b, :], in_=bank[:])
+
         x_in = {}
 
         def load_x(g):
-            xt = xin.tile([P, T4, K], U8, name="x_in")
+            xt = keep.tile([P, T4, K], U8, name="x_in%d" % g)
             nc.sync.dma_start(out=xt[:], in_=xb_v[g])
-            x_in[g] = xt
+            for t in range(T4):
+                x_in[g, t] = xt[:, t, :]
 
+        nc.sync.dma_start(out=sc_rows[0 : K // P, :], in_=x_scale.rearrange("o (m p) -> (o m) p", p=P))
         load_proj(0, 0)
-        nc.sync.dma_start(out=xs[:], in_=x_scale.rearrange("o k -> (o k)").partition_broadcast(P))
-        load_x(0)
-        load_proj(0, 1)
+        for b in range(2):
+            xt = keep.tile([P, 2, K], U8, name="x_in0%d" % b)
+            nc.sync.dma_start(out=xt[:], in_=xb_v[0, :, 2 * b : 2 * b + 2, :])
+            for t in range(2):
+                x_in[0, 2 * b + t] = xt[:, t, :]
+            if b == 0:
+                load_proj(0, 1)
         araw = keep.tile([P, KP, T4, R], BF16, name="araw")
         nc.sync.dma_start(out=araw[:], in_=a.rearrange("(a p j) n -> p a j n", p=P, j=T4))
         load_proj(1, 0)
@@ -121,12 +166,60 @@ def tile_protected_adapter_gradients_s13_kernel(
 
         pgr = {}
 
-        def proj_inter(c, kp, eng):
-            w = keep.tile([P, HALF, T4], BF16, name="pgr%d%d" % (c, kp), align_bytes=64)
-            eng(out=w[:], in_=praw[c, kp][:].rearrange("p j n -> p n j"))
-            pgr[c, kp] = w
+        pt_bank = {}
 
-        def proj_quant(c, kp):
+        def weave(key, planes):
+            bank = ps_mm.tile([P, 2, P, T4], BF16, name="bank_mm")
+            for b in range(2):
+                nc.tensor.matmul(
+                    out=bank[:, b], lhsT=ident16[:], rhs=planes[b].rearrange("p j n -> p n j"), start=True, stop=True
+                )
+            pt_bank[key] = bank
+
+        a_gr = keep.tile([P, KP, R, T4], BF16, name="a_gr", align_bytes=64)
+        for c in range(2):
+            for kp in range(KP):
+                w = keep.tile([P, HALF, T4], BF16, name="pgr%d%d" % (c, kp), align_bytes=64)
+                pgr[c, kp] = w
+
+        def proj_inter(u, eng, part):
+            f = nc.vector.tensor_copy if eng == "V" else nc.scalar.copy
+            if part == "-":
+                c, kp = int(u[0]), int(u[1])
+                f(out=pgr[c, kp][:], in_=praw[c, kp][:].rearrange("p j n -> p n j"))
+            elif u == "a":
+                kp, h = divmod(int(part), 2)
+                n0, n1 = h * P, (h + 1) * P
+                f(out=a_gr[:, kp, n0:n1, :], in_=araw[:, kp, :, n0:n1].rearrange("p j n -> p n j"))
+            else:
+                c, kp = int(u[0]), int(u[1])
+                n0, n1 = int(part) * P, (int(part) + 1) * P
+                f(out=pgr[c, kp][:, n0:n1, :], in_=praw[c, kp][:, :, n0:n1].rearrange("p j n -> p n j"))
+
+        def proj_weave(u, b):
+            if u == "a":
+                weave((u, b), [araw[:, b, :, 128 * i : 128 * (i + 1)] for i in range(2)])
+            else:
+                c, kp = int(u[0]), int(u[1])
+                weave((u, b), [praw[c, kp][:, :, 256 * b + 128 * i : 256 * b + 128 * (i + 1)] for i in range(2)])
+
+        def proj_out(u, b):
+            if u == "a":
+                w = a_gr[:, b]
+            else:
+                c, kp = int(u[0]), int(u[1])
+                w = pgr[c, kp][:, 256 * b : 256 * (b + 1), :]
+            nc.scalar.copy(out=w.rearrange("p (b n) j -> p b n j", b=2), in_=pt_bank[u, b][:])
+
+        def proj_quant(u):
+            if u == "a":
+                nc.vector.quantize_mx(
+                    out=aq[:].rearrange("p a n -> p (a n)").bitcast(E4M3X4),
+                    scales=aqs[:].rearrange("p a n -> p (a n)"),
+                    in_=a_gr[:].rearrange("p a n j -> p (a n j)"),
+                )
+                return
+            c, kp = int(u[0]), int(u[1])
             nc.vector.quantize_mx(
                 out=pq[:, c, kp, :].bitcast(E4M3X4),
                 scales=pqs[:, c, kp, :],
@@ -137,17 +230,22 @@ def tile_protected_adapter_gradients_s13_kernel(
 
         def x_mult(g, t):
             w = xbp.tile([P, K], BF16, name="x_bf")
-            nc.vector.tensor_tensor(out=w[:], in0=x_in[g][:, t, :].bitcast(E4M3), in1=xs[:], op=MULT)
+            nc.vector.tensor_tensor(out=w[:], in0=x_in[g, t].bitcast(E4M3), in1=xs[:].rearrange("p b k -> p (b k)"), op=MULT)
             x_bf[g, t] = w
 
         x_gr = {}
+        tr_bank = {}
 
         def x_turn(g, t):
             bank = ps_tr.tile([P, KP, 2, P], F32, name="bank_tr")
+            tr_bank[g, t] = bank
             words = x_bf[g, t][:].bitcast(F32)
             for kp in range(KP):
                 for u in range(2):
                     nc.tensor.transpose(bank[:, kp, u, :], words[:, 256 * kp + u : 256 * (kp + 1) : 2], ident[:])
+
+        def x_out(g, t):
+            bank = tr_bank[g, t]
             w = xgp.tile([P, KP, P, T4], BF16, name="x_gr", align_bytes=64)
             nc.scalar.copy(
                 out=w[:].rearrange("p a r j -> p (a r j)").bitcast(F32).rearrange("p (a r u) -> p a r u", a=KP, u=2),
@@ -181,16 +279,17 @@ def tile_protected_adapter_gradients_s13_kernel(
 
         z_gr = {}
 
-        def z_out(g):
-            w = grp.tile([P, R, T4], BF16, name="z_gr", align_bytes=64)
-            for h in range(2):
+        def z_out(g, h):
+            if h == 0:
+                z_gr[g] = grp.tile([P, R, T4], BF16, name="z_gr", align_bytes=64)
+            w = z_gr[g]
+            if True:
                 nc.vector.tensor_tensor(
                     out=w[:, h * P : (h + 1) * P, :],
                     in0=z_bank[h][:].rearrange("p t n -> p n t"),
                     in1=r32[:, g : g + 1, :].to_broadcast([P, P, T4]),
                     op=MULT,
                 )
-            z_gr[g] = w
 
         def z_quant(g):
             nc.vector.quantize_mx(
@@ -198,6 +297,7 @@ def tile_protected_adapter_gradients_s13_kernel(
             )
 
         h_pl = {}
+        h_bank = {}
 
         def h_mm(g, t, c):
             bank = ps_mm.tile([P, HALF], F32, name="bank_mm")
@@ -211,104 +311,63 @@ def tile_protected_adapter_gradients_s13_kernel(
                     kp == 0,
                     kp == KP - 1,
                 )
-            if t == 0:
-                h_pl[g, c] = grp.tile([P, T4, HALF], BF16, name="h_pl%d" % c)
+            h_bank[g, t, c] = bank
+
+        def h_out(g, t, c):
+            bank = h_bank[g, t, c]
+            if (g, c) not in h_pl:
+                h_pl[g, c] = hpl.tile([P, T4, HALF], BF16, name="h_pl%d" % c)
             nc.scalar.activation(out=h_pl[g, c][:, t, :], in_=bank[:], func=COPY, scale=r32[:, g, t : t + 1])
 
         h_gr = {}
 
-        def h_inter(g, c):
-            w = grp.tile([P, HALF, T4], BF16, name="h_gr%d" % c, align_bytes=64)
+        def h_inter(g, c, part):
+            if (g, c) not in h_gr:
+                h_gr[g, c] = grp.tile([P, HALF, T4], BF16, name="h_gr%d" % c, align_bytes=64)
+            n0, n1 = {"": (0, HALF), "a": (0, HALF // 2), "b": (HALF // 2, HALF)}[part]
             nc.vector.tensor_copy(
-                out=w[:].rearrange("p (n i) t -> p n t i", i=4),
-                in_=h_pl[g, c][:].rearrange("p t (n i) -> p n t i", i=4),
+                out=h_gr[g, c][:, n0:n1, :].rearrange("p (n i) t -> p n t i", i=4),
+                in_=h_pl[g, c][:, :, n0:n1].rearrange("p t (n i) -> p n t i", i=4),
             )
-            h_gr[g, c] = w
 
-        def h_quant(g, c):
+        def h_quant(g, c, part):
+            n0, n1 = {"": (0, HALF), "a": (0, HALF // 2), "b": (HALF // 2, HALF)}[part]
             nc.vector.quantize_mx(
-                out=hq[:, g, c * HALF : (c + 1) * HALF].bitcast(E4M3X4),
-                scales=hqs[:, g, c * HALF : (c + 1) * HALF],
-                in_=h_gr[g, c][:].rearrange("p n t -> p (n t)"),
+                out=hq[:, g, c * HALF + n0 : c * HALF + n1].bitcast(E4M3X4),
+                scales=hqs[:, g, c * HALF + n0 : c * HALF + n1],
+                in_=h_gr[g, c][:, n0:n1, :].rearrange("p n t -> p (n t)"),
             )
 
-        proj_inter(0, 0, nc.vector.tensor_copy)
-        proj_inter(0, 1, nc.scalar.copy)
-        x_mult(0, 0)
-        x_turn(0, 0)
-        proj_quant(0, 0)
-        x_mult(0, 1)
-        x_turn(0, 1)
-        x_quant(0, 0)
-        proj_quant(0, 1)
-        a_gr = keep.tile([P, KP, R, T4], BF16, name="a_gr", align_bytes=64)
-        nc.vector.tensor_copy(out=a_gr[:], in_=araw[:].rearrange("p a j n -> p a n j"))
-        proj_inter(1, 0, nc.scalar.copy)
-        proj_inter(1, 1, nc.scalar.copy)
-        nc.vector.quantize_mx(
-            out=aq[:].rearrange("p a n -> p (a n)").bitcast(E4M3X4),
-            scales=aqs[:].rearrange("p a n -> p (a n)"),
-            in_=a_gr[:].rearrange("p a n j -> p (a n j)"),
-        )
-        proj_quant(1, 0)
-        proj_quant(1, 1)
+        gb_bank = {}
 
-        steps = [(g, t) for g in range(GROUPS) for t in range(T4)]
-        lead = 6
-        for i in range(2, len(steps) + lead):
-            if i < len(steps):
-                x_mult(*steps[i])
-                x_turn(*steps[i])
-            if 1 <= i - 1 < len(steps):
-                x_quant(*steps[i - 1])
-            j = i - lead
-            if j >= 0:
-                g, t = steps[j]
-                z_mm(g, t)
-                for c in range(2):
-                    h_mm(g, t, c)
-                if t == T4 - 1:
-                    z_out(g)
-                    z_quant(g)
-            j = i - lead - T4
-            if j >= 0:
-                g, t = steps[j]
-                if t == 0:
-                    h_inter(g, 0)
-                elif t == 1:
-                    h_inter(g, 1)
-                elif t == 2:
-                    h_quant(g, 0)
-                else:
-                    h_quant(g, 1)
+        def gb_mm(u):
+            rb, nb = divmod(u, N // HALF)
+            bank = ps_mm.tile([P, HALF], F32, name="bank_mm")
+            for g in range(GROUPS):
+                mx(
+                    bank[:],
+                    zq[:, g, rb * P : (rb + 1) * P],
+                    zqs[:, g, rb * P : (rb + 1) * P],
+                    dw[:, g, 2 * HALF * nb : 2 * HALF * (nb + 1)],
+                    ds[:, g, HALF * nb : HALF * (nb + 1)],
+                    g == 0,
+                    g == GROUPS - 1,
+                    E2M1X4,
+                )
+            gb_bank[u] = bank
 
-        for c in range(2):
-            h_inter(GROUPS - 1, c)
-        for c in range(2):
-            h_quant(GROUPS - 1, c)
+        def gb_out(u, eng):
+            rb, nb = divmod(u, N // HALF)
+            w = outp.tile([P, HALF], F32, name="res")
+            (nc.scalar.copy if eng == "S" else nc.vector.tensor_copy)(out=w[:], in_=gb_bank[u][:])
+            nc.sync.dma_start(out=out_1[rb * P : (rb + 1) * P, nb * HALF : (nb + 1) * HALF], in_=w[:])
 
-        for rb in range(R // P):
-            for nb in range(N // HALF):
-                bank = ps_mm.tile([P, HALF], F32, name="bank_mm")
-                for g in range(GROUPS):
-                    mx(
-                        bank[:],
-                        zq[:, g, rb * P : (rb + 1) * P],
-                        zqs[:, g, rb * P : (rb + 1) * P],
-                        dw[:, g, 2 * HALF * nb : 2 * HALF * (nb + 1)],
-                        ds[:, g, HALF * nb : HALF * (nb + 1)],
-                        g == 0,
-                        g == GROUPS - 1,
-                        E2M1X4,
-                    )
-                w = outp.tile([P, HALF], F32, name="res")
-                nc.scalar.copy(out=w[:], in_=bank[:])
-                nc.sync.dma_start(out=out_1[rb * P : (rb + 1) * P, nb * HALF : (nb + 1) * HALF], in_=w[:])
+        ga_bank = {}
 
-        for kk in range(K // 256):
+        def ga_mm(u):
             bank = ps_mm.tile([P, 2, R], F32, name="bank_mm")
             for b in range(2):
-                k0 = kk * 256 + b * P
+                k0 = u * 256 + b * P
                 for h in range(2):
                     for g in range(GROUPS):
                         mx(
@@ -321,9 +380,53 @@ def tile_protected_adapter_gradients_s13_kernel(
                             g == GROUPS - 1,
                             E2M1X4,
                         )
+            ga_bank[u] = bank
+
+        def ga_out(u, eng):
             w = outp.tile([P, 2, R], F32, name="res")
-            if kk % 2 == 0:
-                nc.scalar.copy(out=w[:], in_=bank[:])
-            else:
-                nc.vector.tensor_copy(out=w[:], in_=bank[:])
-            nc.sync.dma_start(out=out_0[kk * 256 : (kk + 1) * 256, :].rearrange("(b p) n -> p b n", p=P), in_=w[:])
+            (nc.scalar.copy if eng == "S" else nc.vector.tensor_copy)(out=w[:], in_=ga_bank[u][:])
+            nc.sync.dma_start(out=out_0[u * 256 : (u + 1) * 256, :].rearrange("(b p) n -> p b n", p=P), in_=w[:])
+
+        with tc.manual_schedule():
+            for token in ORDER.split():
+                kind, args = token.split(":")[0], token.split(":")[1].split(".")
+                if kind == "PI":
+                    proj_inter(args[0], args[1], args[2])
+                elif kind == "PT":
+                    proj_weave(args[0], int(args[1]))
+                elif kind == "PE":
+                    proj_out(args[0], int(args[1]))
+                elif kind == "PQ":
+                    proj_quant(args[0])
+                elif kind == "XS":
+                    spread_scales()
+                elif kind == "GBO":
+                    gb_out(int(args[0]), args[1])
+                elif kind == "GAO":
+                    ga_out(int(args[0]), args[1])
+                elif kind == "GB":
+                    gb_mm(int(args[0]))
+                elif kind == "GA":
+                    ga_mm(int(args[0]))
+                elif kind == "ZE":
+                    z_out(int(args[0]), int(args[1]))
+                elif kind == "ZQ":
+                    z_quant(int(args[0]))
+                elif kind == "XI":
+                    h_inter(int(args[0]), int(args[1][0]), args[1][1:])
+                elif kind == "HQ":
+                    h_quant(int(args[0]), int(args[1][0]), args[1][1:])
+                elif kind == "H":
+                    h_mm(int(args[0]) // 4, int(args[0]) % 4, int(args[1]))
+                elif kind == "XE":
+                    h_out(int(args[0]) // 4, int(args[0]) % 4, int(args[1]))
+                elif kind == "Z":
+                    z_mm(int(args[0]) // 4, int(args[0]) % 4)
+                elif kind == "XM":
+                    x_mult(int(args[0]) // 4, int(args[0]) % 4)
+                elif kind == "TR":
+                    x_turn(int(args[0]) // 4, int(args[0]) % 4)
+                elif kind == "EV":
+                    x_out(int(args[0]) // 4, int(args[0]) % 4)
+                elif kind == "XQ":
+                    x_quant(int(args[0]) // 4, int(args[0]) % 4)

@@ -26,21 +26,21 @@ HALF = 512
 
 
 ORDER = """
-XS:0 PI:00.V.- PT:01.0 PQ:00 PT:01.1 XM:0 PE:01.0 PE:01.1 XM:1 PI:a.S.0 TR:0 PI:a.S.1 PQ:01 TR:1
-PI:a.S.2 XM:2 PI:a.S.3 EV:0 PQ:a EV:1 XQ:0 TR:2 XM:3 PI:10.S.0 H:0.0 PI:10.S.1 Z:0 XQ:1 PI:10.S.2
-XM:4 H:1.0 PI:10.S.3 Z:1 XM:5 EV:2 TR:3 XE:0.0 TR:4 PQ:10 XE:1.0 XQ:2 EV:3 TR:5 XM:6 EV:4 H:2.0
-PI:11.S.0 Z:2 XQ:3 XQ:4 PI:11.S.1 H:3.0 XM:7 PI:11.S.2 Z:3 H:4.0 PI:11.S.3 ZE:0.0 TR:6 XE:2.0 PQ:11
-TR:7 XE:3.0 ZE:0.1 H:0.1 XE:4.0 XI:0.0 H:1.1 EV:5 H:2.1 XE:0.1 ZQ:0 Z:4 XE:1.1 XQ:5 H:3.1 XM:8
-XE:2.1 Z:5 H:5.0 XE:3.1 H:4.1 XM:9 EV:6 H:5.1 XE:5.0 XQ:6 TR:8 XM:10 XE:4.1 TR:9 XE:5.1 Z:6 XM:11
-EV:7 H:6.0 EV:8 H:6.1 XQ:7 XE:6.0 TR:10 XQ:8 XM:12 XE:6.1 TR:11 EV:9 Z:7 XM:13 H:7.0 EV:10 H:8.0
-EV:11 ZE:1.0 H:7.1 XE:7.0 ZE:1.1 XE:8.0 TR:12 XQ:9 TR:13 XE:7.1 ZQ:1 XQ:10 Z:8 EV:12 XM:14 H:9.0
-EV:13 Z:9 H:8.1 XE:9.0 XQ:11 XI:0.1 Z:10 H:10.0 XE:8.1 Z:11 XE:10.0 H:9.1 XM:15 H:11.0 XE:9.1 H:10.1
-ZE:2.0 XE:11.0 H:11.1 ZE:2.1 XE:10.1 TR:14 XQ:12 XE:11.1 ZQ:2 TR:15 XQ:13 EV:14 XI:1.0 Z:12 H:12.0
-EV:15 Z:13 XE:12.0 H:13.0 XQ:14 XQ:15 Z:14 XI:1.1 XE:13.0 H:12.1 Z:15 XE:12.1 H:14.0 ZE:3.0 H:13.1
-ZE:3.1 XE:14.0 H:15.0 HQ:0.0 XE:13.1 H:14.1 XE:15.0 ZQ:3 H:15.1 HQ:0.1 XE:14.1 GB:0 XI:2.0 XE:15.1
-GB:1 GBO:0.S HQ:1.0 GB:2 HQ:1.1 GBO:1.S XI:2.1 GB:3 GBO:2.S HQ:2.0 GB:4 GBO:3.S HQ:2.1 XI:3.0 GB:5
-GBO:4.S GB:6 XI:3.1a GBO:5.S HQ:3.0 GB:7 GBO:6.S HQ:3.1a XI:3.1b GA:0 GBO:7.S HQ:3.1b GA:1 GAO:0.S
-GA:2 GAO:1.V GA:3 GAO:2.S GAO:3.V
+XS:0 PI:00.V.- PT:01.0 PT:01.1 PE:01.0 PE:01.1 PQ:00 PI:a.S.0 XM:0 XM:1 TR:0 TR:1 PI:a.S.1 PI:a.S.2
+PT:10.0 PI:a.S.3 PQ:01 PE:10.0 EV:0 PT:10.1 PT:11.0 XM:2 EV:1 XM:3 PT:11.1 PE:10.1 XM:4 XQ:0 PE:11.0
+PE:11.1 TR:2 PQ:a EV:2 TR:3 TR:4 XQ:1 EV:3 H:0.0 Z:0 XE:0.0 H:1.0 Z:1 PQ:10 XE:1.0 PQ:11 H:0.1 XQ:2
+XQ:3 XM:5 Z:2 H:1.1 XE:0.1 EV:4 XM:6 XM:7 H:2.0 XM:8 H:3.0 Z:3 XE:2.0 TR:5 TR:6 XE:1.1 H:2.1 EV:5
+H:3.1 TR:7 XM:9 XQ:4 ZE:0.0 TR:8 ZE:0.1 EV:6 TR:9 XE:2.1 XE:3.0 H:4.0 EV:7 EV:8 XQ:5 H:4.1 Z:4 XQ:6
+XQ:7 XE:3.1 XE:4.0 H:5.0 XM:10 Z:5 XE:4.1 H:6.0 Z:6 H:5.1 Z:7 EV:9 XM:11 TR:10 XE:5.0 TR:11 XE:5.1
+XM:12 ZE:1.0 XM:13 XQ:8 EV:10 ZE:1.1 EV:11 XQ:9 TR:12 H:7.0 XE:6.0 H:6.1 XE:7.0 H:7.1 ZQ:0 XE:6.1
+XQ:10 H:8.1 Z:8 ZQ:1 H:9.1 Z:9 XE:7.1 EV:12 XE:8.1 XE:9.1 H:10.1 XM:14 XQ:11 Z:10 XE:10.1 H:8.0
+XE:8.0 XQ:12 Z:11 H:11.1 H:9.0 XM:15 ZE:2.0 TR:13 XE:9.0 EV:13 XE:11.1 TR:14 XI:0.0 ZE:2.1 XQ:13
+EV:14 TR:15 H:10.0 Z:12 H:11.0 XE:10.0 EV:15 Z:13 XQ:14 H:12.0 Z:14 XE:11.0 ZQ:2 XE:12.0 H:13.0
+XQ:15 Z:15 H:12.1 H:14.0 XE:13.0 XI:0.1 H:13.1 XE:12.1 ZE:3.0 XE:14.0 H:15.0 ZE:3.1 XE:13.1 XE:15.0
+HQ:0.0 H:14.1 ZQ:3 XE:14.1 GB:0 HQ:0.1 GBO:0.S GB:1 H:15.1 XI:1.0 GB:2 GBO:1.S XE:15.1 XI:2.1.0
+GBO:2.S GB:3 XI:2.1.1 XI:2.0 HQ:1.0 HQ:2.0 GB:4 XI:2.1.2 GB:5 GBO:3.S GBO:4.S XI:3.0 GBO:5.S GB:6
+HQ:3.0 GA:0 XI:1.1 XI:2.1.3 GB:7 HQ:1.1 GAO:0.S GA:1 XI:3.1a GBO:6.S XI:3.1b HQ:2.1 HQ:3.1a GA:2
+HQ:3.1b GBO:7.S GA:3a GA:3b GAO:1.V GAO:2.S GAO:3a.V GAO:3b.S
 """
 
 
@@ -324,8 +324,13 @@ def tile_protected_adapter_gradients_s13_kernel(
         def h_inter(g, c, part):
             if (g, c) not in h_gr:
                 h_gr[g, c] = grp.tile([P, HALF, T4], BF16, name="h_gr%d" % c, align_bytes=64)
-            n0, n1 = {"": (0, HALF), "a": (0, HALF // 2), "b": (HALF // 2, HALF)}[part]
-            nc.vector.tensor_copy(
+            f = nc.vector.tensor_copy
+            if part in "0123" and part:
+                f = nc.scalar.copy
+                n0, n1 = int(part) * P, (int(part) + 1) * P
+            else:
+                n0, n1 = {"": (0, HALF), "a": (0, HALF // 2), "b": (HALF // 2, HALF)}[part]
+            f(
                 out=h_gr[g, c][:, n0:n1, :].rearrange("p (n i) t -> p n t i", i=4),
                 in_=h_pl[g, c][:, :, n0:n1].rearrange("p t (n i) -> p n t i", i=4),
             )
@@ -364,16 +369,20 @@ def tile_protected_adapter_gradients_s13_kernel(
 
         ga_bank = {}
 
+        def ga_blocks(u):
+            k0 = int(u[0]) * 2
+            return {"": [k0, k0 + 1], "a": [k0], "b": [k0 + 1]}[u[1:]]
+
         def ga_mm(u):
-            bank = ps_mm.tile([P, 2, R], F32, name="bank_mm")
-            for b in range(2):
-                k0 = u * 256 + b * P
+            blocks = ga_blocks(u)
+            bank = ps_mm.tile([P, len(blocks), R], F32, name="bank_mm")
+            for b, kb in enumerate(blocks):
                 for h in range(2):
                     for g in range(GROUPS):
                         mx(
                             bank[:, b, h * P : (h + 1) * P],
-                            hq[:, g, k0 : k0 + P],
-                            hqs[:, g, k0 : k0 + P],
+                            hq[:, g, kb * P : (kb + 1) * P],
+                            hqs[:, g, kb * P : (kb + 1) * P],
                             ew[:, g, 2 * P * h : 2 * P * (h + 1)],
                             es[:, g, P * h : P * (h + 1)],
                             g == 0,
@@ -383,9 +392,12 @@ def tile_protected_adapter_gradients_s13_kernel(
             ga_bank[u] = bank
 
         def ga_out(u, eng):
-            w = outp.tile([P, 2, R], F32, name="res")
+            blocks = ga_blocks(u)
+            w = outp.tile([P, len(blocks), R], F32, name="res")
             (nc.scalar.copy if eng == "S" else nc.vector.tensor_copy)(out=w[:], in_=ga_bank[u][:])
-            nc.sync.dma_start(out=out_0[u * 256 : (u + 1) * 256, :].rearrange("(b p) n -> p b n", p=P), in_=w[:])
+            nc.sync.dma_start(
+                out=out_0[blocks[0] * P : (blocks[-1] + 1) * P, :].rearrange("(b p) n -> p b n", p=P), in_=w[:]
+            )
 
         with tc.manual_schedule():
             for token in ORDER.split():
@@ -403,17 +415,17 @@ def tile_protected_adapter_gradients_s13_kernel(
                 elif kind == "GBO":
                     gb_out(int(args[0]), args[1])
                 elif kind == "GAO":
-                    ga_out(int(args[0]), args[1])
+                    ga_out(args[0], args[1])
                 elif kind == "GB":
                     gb_mm(int(args[0]))
                 elif kind == "GA":
-                    ga_mm(int(args[0]))
+                    ga_mm(args[0])
                 elif kind == "ZE":
                     z_out(int(args[0]), int(args[1]))
                 elif kind == "ZQ":
                     z_quant(int(args[0]))
                 elif kind == "XI":
-                    h_inter(int(args[0]), int(args[1][0]), args[1][1:])
+                    h_inter(int(args[0]), int(args[1][0]), args[1][1:] + "".join(args[2:]))
                 elif kind == "HQ":
                     h_quant(int(args[0]), int(args[1][0]), args[1][1:])
                 elif kind == "H":

from contextlib import ExitStack

import concourse.mybir as mybir
from concourse.masks import make_identity

M, K, N, R = 2048, 1024, 2048, 256
FLOPS = 2 * M * K * (K + R) + 2 * K * M * R + 2 * R * M * N

F32 = mybir.dt.float32
BF16 = mybir.dt.bfloat16
I32 = mybir.dt.int32
U32 = mybir.dt.uint32
U8 = mybir.dt.uint8
E4M3 = mybir.dt.float8_e4m3fn
E4M3X4 = mybir.dt.float8_e4m3fn_x4
E2M1X4 = mybir.dt.float4_e2m1fn_x4
MULT = mybir.AluOpType.mult
COPY = mybir.ActivationFunctionType.Copy

P = 128
T4 = 4
GROUP = P * T4
GROUPS = M // GROUP
KP = K // GROUP
HALF = 512


ORDER = """
XS:0 PI:00.V.- PT:01.0 PT:01.1 PE:01.0 PE:01.1 PQ:00 PI:a.S.0 XM:0 XM:1 TR:0 TR:1 PI:a.S.1 PI:a.S.2
PT:10.0 PI:a.S.3 PQ:01 PE:10.0 EV:0 PT:10.1 PT:11.0 XM:2 EV:1 XM:3 PT:11.1 PE:10.1 XM:4 XQ:0 PE:11.0
PE:11.1 TR:2 PQ:a EV:2 TR:3 TR:4 XQ:1 EV:3 H:0.0 Z:0 XE:0.0 H:1.0 Z:1 PQ:10 XE:1.0 PQ:11 H:0.1 XQ:2
XQ:3 XM:5 Z:2 H:1.1 XE:0.1 EV:4 XM:6 XM:7 H:2.0 XM:8 H:3.0 Z:3 XE:2.0 TR:5 TR:6 XE:1.1 H:2.1 EV:5
H:3.1 TR:7 XM:9 XQ:4 ZE:0.0 TR:8 ZE:0.1 EV:6 TR:9 XE:2.1 XE:3.0 H:4.0 EV:7 EV:8 XQ:5 H:4.1 Z:4 XQ:6
XQ:7 XE:3.1 XE:4.0 H:5.0 XM:10 Z:5 XE:4.1 H:6.0 Z:6 H:5.1 Z:7 EV:9 XM:11 TR:10 XE:5.0 TR:11 XE:5.1
XM:12 ZE:1.0 XM:13 XQ:8 EV:10 ZE:1.1 EV:11 XQ:9 TR:12 H:7.0 XE:6.0 H:6.1 XE:7.0 H:7.1 ZQ:0 XE:6.1
XQ:10 H:8.1 Z:8 ZQ:1 H:9.1 Z:9 XE:7.1 EV:12 XE:8.1 XE:9.1 H:10.1 XM:14 XQ:11 Z:10 XE:10.1 H:8.0
XE:8.0 XQ:12 Z:11 H:11.1 H:9.0 XM:15 ZE:2.0 TR:13 XE:9.0 EV:13 XE:11.1 TR:14 XI:0.0 ZE:2.1 XQ:13
EV:14 TR:15 H:10.0 Z:12 H:11.0 XE:10.0 EV:15 Z:13 XQ:14 H:12.0 Z:14 XE:11.0 ZQ:2 XE:12.0 H:13.0
XQ:15 Z:15 H:12.1 H:14.0 XE:13.0 XI:0.1 H:13.1 XE:12.1 ZE:3.0 XE:14.0 H:15.0 ZE:3.1 XE:13.1 XE:15.0
HQ:0.0 H:14.1 ZQ:3 XE:14.1 GB:0 HQ:0.1 GBO:0.S GB:1 H:15.1 XI:1.0 GB:2 GBO:1.S XE:15.1 XI:2.1.0
GBO:2.S GB:3 XI:2.1.1 XI:2.0 HQ:1.0 HQ:2.0 GB:4 XI:2.1.2 GB:5 GBO:3.S GBO:4.S XI:3.0 GBO:5.S GB:6
HQ:3.0 GA:0 XI:1.1 XI:2.1.3 GB:7 HQ:1.1 GAO:0.S GA:1 XI:3.1a GBO:6.S XI:3.1b HQ:2.1 HQ:3.1a GA:2
HQ:3.1b GBO:7.S GA:3a GA:3b GAO:1.V GAO:2.S GAO:3a.V GAO:3b.S
"""


def tile_protected_adapter_gradients_s13_kernel(
    tc, x_bytes, x_scale, proj, a, r, e_words, e_scales, d_words, d_scales, out_0, out_1
):
    nc = tc.nc
    with ExitStack() as ctx:
        keep = ctx.enter_context(tc.tile_pool(name="keep", bufs=1))
        xbp = ctx.enter_context(tc.tile_pool(name="xbp", bufs=8))
        xgp = ctx.enter_context(tc.tile_pool(name="xgp", bufs=8))
        hpl = ctx.enter_context(tc.tile_pool(name="hpl", bufs=3))
        grp = ctx.enter_context(tc.tile_pool(name="grp", bufs=2))
        outp = ctx.enter_context(tc.tile_pool(name="outp", bufs=6))
        ps_tr = ctx.enter_context(tc.psum_pool(name="ps_tr", bufs=3))
        ps_z = ctx.enter_context(tc.psum_pool(name="ps_z", bufs=1))
        ps_mm = ctx.enter_context(tc.psum_pool(name="ps_mm", bufs=3))

        warm = keep.tile([P, 1], F32, name="warm")
        nc.gpsimd.memset(warm[:], 0.0)
        nc.scalar.activation(out=warm[:], in_=warm[:], func=COPY)
        ident = keep.tile([P, P], F32, name="ident")
        make_identity(nc, ident[:])
        ident16 = keep.tile([P, P], BF16, name="ident16")
        nc.gpsimd.tensor_copy(out=ident16[:], in_=ident[:])
        es = keep.tile([P, GROUPS, R], U8, name="es", align_bytes=64)
        ds = keep.tile([P, GROUPS, N], U8, name="ds", align_bytes=64)
        nc.gpsimd.memset(es[:].rearrange("p g n -> p (g n)").bitcast(I32), 0)
        nc.gpsimd.memset(ds[:].rearrange("p g n -> p (g n)").bitcast(I32), 0)

        sc_rows = keep.tile([P, P], F32, name="sc_rows")
        nc.vector.memset(sc_rows[:], 0.0)

        r16 = keep.tile([P, GROUPS, T4], BF16, name="r16")
        nc.scalar.dma_start(out=r16[:], in_=r.rearrange("(g p t) -> p g t", p=P, t=T4))
        r32 = keep.tile([P, GROUPS, T4], F32, name="r32")
        nc.gpsimd.tensor_copy(out=r32[:], in_=r16[:])

        proj_v = proj.rearrange("(a p j) n -> a p j n", p=P, j=T4)
        xb_v = x_bytes.rearrange("(g p t) k -> g p t k", p=P, t=T4)
        praw = {}

        def load_proj(c, kp):
            w = keep.tile([P, T4, HALF], BF16, name="praw%d%d" % (c, kp))
            nc.sync.dma_start(out=w[:], in_=proj_v[kp, :, :, c * HALF : (c + 1) * HALF])
            praw[c, kp] = w

        xs = keep.tile([P, 2, HALF], F32, name="xs")
        sc_col = keep.tile([P, K // P], F32, name="sc_col")

        def spread_scales():
            bank = ps_tr.tile([P, P], F32, name="bank_tr")
            nc.tensor.transpose(bank[:], sc_rows[:], ident[:])
            nc.scalar.copy(out=sc_col[:], in_=bank[:, 0 : K // P])
            for b in range(2):
                bank = ps_mm.tile([P, HALF], F32, name="bank_mm")
                for j in range(HALF // P):
                    m = b * (HALF // P) + j
                    nc.tensor.transpose(
                        bank[:, j * P : (j + 1) * P], sc_col[:, m : m + 1].to_broadcast([P, P]), ident[:]
                    )
                nc.scalar.copy(out=xs[:, b, :], in_=bank[:])

        x_in = {}

        def load_x(g):
            xt = keep.tile([P, T4, K], U8, name="x_in%d" % g)
            nc.sync.dma_start(out=xt[:], in_=xb_v[g])
            for t in range(T4):
                x_in[g, t] = xt[:, t, :]

        nc.sync.dma_start(out=sc_rows[0 : K // P, :], in_=x_scale.rearrange("o (m p) -> (o m) p", p=P))
        load_proj(0, 0)
        for b in range(2):
            xt = keep.tile([P, 2, K], U8, name="x_in0%d" % b)
            nc.sync.dma_start(out=xt[:], in_=xb_v[0, :, 2 * b : 2 * b + 2, :])
            for t in range(2):
                x_in[0, 2 * b + t] = xt[:, t, :]
            if b == 0:
                load_proj(0, 1)
        araw = keep.tile([P, KP, T4, R], BF16, name="araw")
        nc.sync.dma_start(out=araw[:], in_=a.rearrange("(a p j) n -> p a j n", p=P, j=T4))
        load_proj(1, 0)
        load_proj(1, 1)
        for g in range(1, GROUPS):
            load_x(g)
        ew = keep.tile([P, GROUPS, 2 * R], U8, name="ew", align_bytes=64)
        dw = keep.tile([P, GROUPS, 2 * N], U8, name="dw", align_bytes=64)
        for g in range(GROUPS):
            nc.sync.dma_start(out=dw[:, g, :].bitcast(I32), in_=d_words[g].bitcast(I32))
        nc.sync.dma_start(out=ew[:].bitcast(I32), in_=e_words.bitcast(I32).rearrange("g p n -> p g n"))
        for q in range(4):
            nc.sync.dma_start(
                out=ds[32 * q : 32 * q + 4].bitcast(I32),
                in_=d_scales[:, 4 * q : 4 * q + 4, :].bitcast(I32).rearrange("g q n -> q g n"),
            )
            nc.sync.dma_start(
                out=es[32 * q : 32 * q + 4].bitcast(I32),
                in_=e_scales[:, 4 * q : 4 * q + 4, :].bitcast(I32).rearrange("g q n -> q g n"),
            )

        pq = keep.tile([P, 2, KP, HALF], U32, name="pq", align_bytes=64)
        pqs = keep.tile([P, 2, KP, HALF], U8, name="pqs", align_bytes=64)
        aq = keep.tile([P, KP, R], U32, name="aq", align_bytes=64)
        aqs = keep.tile([P, KP, R], U8, name="aqs", align_bytes=64)
        xq = keep.tile([P, GROUPS, T4, KP, P], U32, name="xq", align_bytes=64)
        xqs = keep.tile([P, GROUPS, T4, KP, P], U8, name="xqs", align_bytes=64)
        zq = keep.tile([P, GROUPS, R], U32, name="zq", align_bytes=64)
        zqs = keep.tile([P, GROUPS, R], U8, name="zqs", align_bytes=64)
        hq = keep.tile([P, GROUPS, K], U32, name="hq", align_bytes=64)
        hqs = keep.tile([P, GROUPS, K], U8, name="hqs", align_bytes=64)

        def mx(out, lhs, lhs_s, rhs, rhs_s, start, stop, rdt=E4M3X4):
            nc.tensor.matmul_mx(
                out=out,
                lhsT=lhs.bitcast(E4M3X4),
                lhsT_scale=lhs_s,
                rhs=rhs.bitcast(rdt),
                rhs_scale=rhs_s,
                start=start,
                stop=stop,
            )

        pgr = {}

        pt_bank = {}

        def weave(key, planes):
            bank = ps_mm.tile([P, 2, P, T4], BF16, name="bank_mm")
            for b in range(2):
                nc.tensor.matmul(
                    out=bank[:, b], lhsT=ident16[:], rhs=planes[b].rearrange("p j n -> p n j"), start=True, stop=True
                )
            pt_bank[key] = bank

        a_gr = keep.tile([P, KP, R, T4], BF16, name="a_gr", align_bytes=64)
        for c in range(2):
            for kp in range(KP):
                w = keep.tile([P, HALF, T4], BF16, name="pgr%d%d" % (c, kp), align_bytes=64)
                pgr[c, kp] = w

        def proj_inter(u, eng, part):
            f = nc.vector.tensor_copy if eng == "V" else nc.scalar.copy
            if part == "-":
                c, kp = int(u[0]), int(u[1])
                f(out=pgr[c, kp][:], in_=praw[c, kp][:].rearrange("p j n -> p n j"))
            elif u == "a":
                kp, h = divmod(int(part), 2)
                n0, n1 = h * P, (h + 1) * P
                f(out=a_gr[:, kp, n0:n1, :], in_=araw[:, kp, :, n0:n1].rearrange("p j n -> p n j"))
            else:
                c, kp = int(u[0]), int(u[1])
                n0, n1 = int(part) * P, (int(part) + 1) * P
                f(out=pgr[c, kp][:, n0:n1, :], in_=praw[c, kp][:, :, n0:n1].rearrange("p j n -> p n j"))

        def proj_weave(u, b):
            if u == "a":
                weave((u, b), [araw[:, b, :, 128 * i : 128 * (i + 1)] for i in range(2)])
            else:
                c, kp = int(u[0]), int(u[1])
                weave((u, b), [praw[c, kp][:, :, 256 * b + 128 * i : 256 * b + 128 * (i + 1)] for i in range(2)])

        def proj_out(u, b):
            if u == "a":
                w = a_gr[:, b]
            else:
                c, kp = int(u[0]), int(u[1])
                w = pgr[c, kp][:, 256 * b : 256 * (b + 1), :]
            nc.scalar.copy(out=w.rearrange("p (b n) j -> p b n j", b=2), in_=pt_bank[u, b][:])

        def proj_quant(u):
            if u == "a":
                nc.vector.quantize_mx(
                    out=aq[:].rearrange("p a n -> p (a n)").bitcast(E4M3X4),
                    scales=aqs[:].rearrange("p a n -> p (a n)"),
                    in_=a_gr[:].rearrange("p a n j -> p (a n j)"),
                )
                return
            c, kp = int(u[0]), int(u[1])
            nc.vector.quantize_mx(
                out=pq[:, c, kp, :].bitcast(E4M3X4),
                scales=pqs[:, c, kp, :],
                in_=pgr[c, kp][:].rearrange("p n j -> p (n j)"),
            )

        x_bf = {}

        def x_mult(g, t):
            w = xbp.tile([P, K], BF16, name="x_bf")
            nc.vector.tensor_tensor(out=w[:], in0=x_in[g, t].bitcast(E4M3), in1=xs[:].rearrange("p b k -> p (b k)"), op=MULT)
            x_bf[g, t] = w

        x_gr = {}
        tr_bank = {}

        def x_turn(g, t):
            bank = ps_tr.tile([P, KP, 2, P], F32, name="bank_tr")
            tr_bank[g, t] = bank
            words = x_bf[g, t][:].bitcast(F32)
            for kp in range(KP):
                for u in range(2):
                    nc.tensor.transpose(bank[:, kp, u, :], words[:, 256 * kp + u : 256 * (kp + 1) : 2], ident[:])

        def x_out(g, t):
            bank = tr_bank[g, t]
            w = xgp.tile([P, KP, P, T4], BF16, name="x_gr", align_bytes=64)
            nc.scalar.copy(
                out=w[:].rearrange("p a r j -> p (a r j)").bitcast(F32).rearrange("p (a r u) -> p a r u", a=KP, u=2),
                in_=bank[:].rearrange("p a u r -> p a r u"),
            )
            x_gr[g, t] = w

        def x_quant(g, t):
            nc.vector.quantize_mx(
                out=xq[:, g, t].rearrange("p a r -> p (a r)").bitcast(E4M3X4),
                scales=xqs[:, g, t].rearrange("p a r -> p (a r)"),
                in_=x_gr[g, t][:].rearrange("p a r j -> p (a r j)"),
            )

        z_bank = {}

        def z_mm(g, t):
            for h in range(2):
                if t == 0:
                    z_bank[h] = ps_z.tile([P, T4, P], F32, name="z_bank%d" % h)
                for kp in range(KP):
                    mx(
                        z_bank[h][:, t, :],
                        xq[:, g, t, kp, :],
                        xqs[:, g, t, kp, :],
                        aq[:, kp, h * P : (h + 1) * P],
                        aqs[:, kp, h * P : (h + 1) * P],
                        kp == 0,
                        kp == KP - 1,
                    )

        z_gr = {}

        def z_out(g, h):
            if h == 0:
                z_gr[g] = grp.tile([P, R, T4], BF16, name="z_gr", align_bytes=64)
            w = z_gr[g]
            if True:
                nc.vector.tensor_tensor(
                    out=w[:, h * P : (h + 1) * P, :],
                    in0=z_bank[h][:].rearrange("p t n -> p n t"),
                    in1=r32[:, g : g + 1, :].to_broadcast([P, P, T4]),
                    op=MULT,
                )

        def z_quant(g):
            nc.vector.quantize_mx(
                out=zq[:, g, :].bitcast(E4M3X4), scales=zqs[:, g, :], in_=z_gr[g][:].rearrange("p n t -> p (n t)")
            )

        h_pl = {}
        h_bank = {}

        def h_mm(g, t, c):
            bank = ps_mm.tile([P, HALF], F32, name="bank_mm")
            for kp in range(KP):
                mx(
                    bank[:],
                    xq[:, g, t, kp, :],
                    xqs[:, g, t, kp, :],
                    pq[:, c, kp, :],
                    pqs[:, c, kp, :],
                    kp == 0,
                    kp == KP - 1,
                )
            h_bank[g, t, c] = bank

        def h_out(g, t, c):
            bank = h_bank[g, t, c]
            if (g, c) not in h_pl:
                h_pl[g, c] = hpl.tile([P, T4, HALF], BF16, name="h_pl%d" % c)
            nc.scalar.activation(out=h_pl[g, c][:, t, :], in_=bank[:], func=COPY, scale=r32[:, g, t : t + 1])

        h_gr = {}

        def h_inter(g, c, part):
            if (g, c) not in h_gr:
                h_gr[g, c] = grp.tile([P, HALF, T4], BF16, name="h_gr%d" % c, align_bytes=64)
            f = nc.vector.tensor_copy
            if part in "0123" and part:
                f = nc.scalar.copy
                n0, n1 = int(part) * P, (int(part) + 1) * P
            else:
                n0, n1 = {"": (0, HALF), "a": (0, HALF // 2), "b": (HALF // 2, HALF)}[part]
            f(
                out=h_gr[g, c][:, n0:n1, :].rearrange("p (n i) t -> p n t i", i=4),
                in_=h_pl[g, c][:, :, n0:n1].rearrange("p t (n i) -> p n t i", i=4),
            )

        def h_quant(g, c, part):
            n0, n1 = {"": (0, HALF), "a": (0, HALF // 2), "b": (HALF // 2, HALF)}[part]
            nc.vector.quantize_mx(
                out=hq[:, g, c * HALF + n0 : c * HALF + n1].bitcast(E4M3X4),
                scales=hqs[:, g, c * HALF + n0 : c * HALF + n1],
                in_=h_gr[g, c][:, n0:n1, :].rearrange("p n t -> p (n t)"),
            )

        gb_bank = {}

        def gb_mm(u):
            rb, nb = divmod(u, N // HALF)
            bank = ps_mm.tile([P, HALF], F32, name="bank_mm")
            for g in range(GROUPS):
                mx(
                    bank[:],
                    zq[:, g, rb * P : (rb + 1) * P],
                    zqs[:, g, rb * P : (rb + 1) * P],
                    dw[:, g, 2 * HALF * nb : 2 * HALF * (nb + 1)],
                    ds[:, g, HALF * nb : HALF * (nb + 1)],
                    g == 0,
                    g == GROUPS - 1,
                    E2M1X4,
                )
            gb_bank[u] = bank

        def gb_out(u, eng):
            rb, nb = divmod(u, N // HALF)
            w = outp.tile([P, HALF], F32, name="res")
            (nc.scalar.copy if eng == "S" else nc.vector.tensor_copy)(out=w[:], in_=gb_bank[u][:])
            nc.sync.dma_start(out=out_1[rb * P : (rb + 1) * P, nb * HALF : (nb + 1) * HALF], in_=w[:])

        ga_bank = {}

        def ga_blocks(u):
            k0 = int(u[0]) * 2
            return {"": [k0, k0 + 1], "a": [k0], "b": [k0 + 1]}[u[1:]]

        def ga_mm(u):
            blocks = ga_blocks(u)
            bank = ps_mm.tile([P, len(blocks), R], F32, name="bank_mm")
            for b, kb in enumerate(blocks):
                for h in range(2):
                    for g in range(GROUPS):
                        mx(
                            bank[:, b, h * P : (h + 1) * P],
                            hq[:, g, kb * P : (kb + 1) * P],
                            hqs[:, g, kb * P : (kb + 1) * P],
                            ew[:, g, 2 * P * h : 2 * P * (h + 1)],
                            es[:, g, P * h : P * (h + 1)],
                            g == 0,
                            g == GROUPS - 1,
                            E2M1X4,
                        )
            ga_bank[u] = bank

        def ga_out(u, eng):
            blocks = ga_blocks(u)
            w = outp.tile([P, len(blocks), R], F32, name="res")
            (nc.scalar.copy if eng == "S" else nc.vector.tensor_copy)(out=w[:], in_=ga_bank[u][:])
            nc.sync.dma_start(
                out=out_0[blocks[0] * P : (blocks[-1] + 1) * P, :].rearrange("(b p) n -> p b n", p=P), in_=w[:]
            )

        with tc.manual_schedule():
            for token in ORDER.split():
                kind, args = token.split(":")[0], token.split(":")[1].split(".")
                if kind == "PI":
                    proj_inter(args[0], args[1], args[2])
                elif kind == "PT":
                    proj_weave(args[0], int(args[1]))
                elif kind == "PE":
                    proj_out(args[0], int(args[1]))
                elif kind == "PQ":
                    proj_quant(args[0])
                elif kind == "XS":
                    spread_scales()
                elif kind == "GBO":
                    gb_out(int(args[0]), args[1])
                elif kind == "GAO":
                    ga_out(args[0], args[1])
                elif kind == "GB":
                    gb_mm(int(args[0]))
                elif kind == "GA":
                    ga_mm(args[0])
                elif kind == "ZE":
                    z_out(int(args[0]), int(args[1]))
                elif kind == "ZQ":
                    z_quant(int(args[0]))
                elif kind == "XI":
                    h_inter(int(args[0]), int(args[1][0]), args[1][1:] + "".join(args[2:]))
                elif kind == "HQ":
                    h_quant(int(args[0]), int(args[1][0]), args[1][1:])
                elif kind == "H":
                    h_mm(int(args[0]) // 4, int(args[0]) % 4, int(args[1]))
                elif kind == "XE":
                    h_out(int(args[0]) // 4, int(args[0]) % 4, int(args[1]))
                elif kind == "Z":
                    z_mm(int(args[0]) // 4, int(args[0]) % 4)
                elif kind == "XM":
                    x_mult(int(args[0]) // 4, int(args[0]) % 4)
                elif kind == "TR":
                    x_turn(int(args[0]) // 4, int(args[0]) % 4)
                elif kind == "EV":
                    x_out(int(args[0]) // 4, int(args[0]) % 4)
                elif kind == "XQ":
                    x_quant(int(args[0]) // 4, int(args[0]) % 4)
